import numpy as np
import ml_dtypes


def mxq(x, axis, fmt="e4m3"):
    dtype, down = {"e4m3": (ml_dtypes.float8_e4m3fn, 7), "e5m2": (ml_dtypes.float8_e5m2, 14)}[fmt]
    v = np.moveaxis(np.asarray(x, np.float32).astype(ml_dtypes.bfloat16).astype(np.float64), axis, -1)
    blocks = v.reshape(v.shape[:-1] + (-1, 32))
    amax = np.abs(blocks).max(-1, keepdims=True)
    byte = np.maximum(np.where(amax > 0, np.frexp(amax)[1] - 1 + 127, 0) - down, 1)
    scale = np.exp2(byte - 127.0)
    codes = (blocks / scale).astype(np.float32).astype(dtype).astype(np.float64)
    return np.moveaxis((codes * scale).reshape(v.shape), -1, axis)


WIDE = False


def mx_kscale(k):
    if not WIDE:
        return np.ones(k)
    levels = np.array([10, -10, 5, -5, 0])
    if k % 512:
        return np.exp2(np.random.permutation(np.resize(levels, k // 32))).repeat(32)
    a = np.empty((k // 512, 16))
    for p in range(k // 512):
        a[p, :8] = np.random.permutation(np.resize(levels, 8))
        for g in range(8):
            far = levels[np.abs(levels - a[p, g]) >= 10]
            a[p, g + 8] = far[np.random.randint(len(far))]
    return np.exp2(a.ravel()).repeat(32)


BF16 = ml_dtypes.bfloat16


def bf(x):
    return np.asarray(x, np.float32).astype(BF16)


def f64(x):
    return np.asarray(x).astype(np.float64)


E2M1 = np.array([0.0, 0.5, 1.0, 1.5, 2.0, 3.0, 4.0, 6.0, -0.0, -0.5, -1.0, -1.5, -2.0, -3.0, -4.0, -6.0])


def pack_weight(w, fmt):
    k, n = w.shape
    w = f64(bf(w)).reshape(k // 32, 32, n)
    amax = np.abs(w).max(1)
    if fmt == "e4m3":
        byte = np.frexp(amax)[1] - 1 + 127 - 7
    else:
        mant, ex = np.frexp(amax / 6.0)
        byte = np.where(mant > 0.5, ex, ex - 1) + 127
    byte = np.clip(np.where(amax > 0, byte, 1), 1, 254)
    scaled = (w * np.exp2(127.0 - byte)[:, None, :]).reshape(k, n).astype(np.float32)
    by_word = np.ascontiguousarray(scaled.reshape(k // 512, 128, 4, n).transpose(0, 1, 3, 2))
    if fmt == "e4m3":
        words = by_word.astype(ml_dtypes.float8_e4m3fn).view(np.uint8)
    else:
        c = by_word.astype(ml_dtypes.float4_e2m1fn).view(np.uint8) & 0xF
        words = c[..., 0::2] | (c[..., 1::2] << 4)
    return np.ascontiguousarray(words), np.ascontiguousarray(byte.astype(np.uint8).reshape(k // 512, 16, n))


def unpack_weight(words, scales, fmt):
    g, p, n, _ = words.shape
    if fmt == "e4m3":
        vals = np.ascontiguousarray(words).view(ml_dtypes.float8_e4m3fn).astype(np.float64)
    else:
        nib = np.empty((g, p, n, 4), np.uint8)
        nib[..., 0::2] = words & 0xF
        nib[..., 1::2] = words >> 4
        vals = E2M1[nib]
    vals = vals * np.repeat(np.exp2(scales.astype(np.float64) - 127.0), 8, axis=1)[..., None]
    return vals.transpose(0, 1, 3, 2).reshape(g * 512, n)
def pack4(w):
    words, scales = pack_weight(w, "e2m1")
    return words.reshape(words.shape[0], 128, -1), scales


def unpack4(words, scales):
    return unpack_weight(words.reshape(words.shape[0], 128, -1, 2), scales, "e2m1")


E4M3FN = np.array([(-1.0 if i & 128 else 1.0) * ((1.0 + (i & 7) / 8.0) * 2.0 ** (((i >> 3) & 15) - 7) if i & 120 else (i & 7) * 2.0 ** -9) for i in range(256)])


def e4m3fn_bytes(y):
    return np.clip(np.asarray(y, np.float64), -448.0, 448.0).astype(np.float32).astype(ml_dtypes.float8_e4m3fn).view(np.uint8)


def e4m3fn_values(b):
    return E4M3FN[b]


N, D, F, R = 2048, 1024, 1024, 256

SCALE = 2.0


def draw0():
    s, t, r = mx_kscale(N), mx_kscale(F), mx_kscale(D)
    mean = N ** -0.25
    x = bf((mean + np.random.standard_normal((N, D))) * s[:, None])
    g = bf((mean + np.random.standard_normal((N, F))) / s[:, None])
    v = bf((0.5 + np.random.standard_normal((D, F))) / np.sqrt(D))
    m = bf(np.random.uniform(0.5, 1.5, (F,)) * t)
    p = bf((1.0 + 0.1 * np.random.standard_normal(D)) * r)
    a_words, a_scales = pack4(np.random.standard_normal((D, R)) / np.sqrt(D) / r[:, None])
    b_words, b_scales = pack4((np.random.standard_normal((R, F)) / np.sqrt(F) / t[None, :]).T)
    return {
        "x": x,
        "g": g,
        "v": v,
        "m": m,
        "p": p,
        "a_words": a_words,
        "a_scales": a_scales,
        "b_words": b_words,
        "b_scales": b_scales,
    }


def column_norm_backward(dweff, v):
    c2 = np.sum(v * v, axis=0)
    c = np.sqrt(c2)
    proj = np.sum(dweff * v, axis=0) / c2
    return (dweff - v * proj[None, :]) / c[None, :]


def core(x, g, v, m, p, a_words, a_scales, b_words, b_scales):
    x, g, v, m, p = f64(x), f64(g), f64(v), f64(m), f64(p)
    a = unpack4(a_words, a_scales)
    bt = unpack4(b_words, b_scales)
    root_n = np.sqrt(x.shape[0])

    dweff = (mxq(x, 0, "e4m3").T @ mxq(g, 0, "e4m3")) / root_n

    u = column_norm_backward(dweff, v)

    dv = u * m[None, :]
    da = SCALE * (mxq(dv, 1, "e4m3") @ bt)

    up = p[:, None] * u
    db = SCALE * (a.T @ mxq(up, 0, "e4m3"))

    return da, db


def setup_inputs():
    drawn = draw0()
    full = np.asarray(drawn['x']).astype(np.float64)
    scale = (np.abs(full).reshape(2048, 8, 128).max(axis=(2,)) / 448.0).astype(np.float32)
    given = {}
    for key, value in drawn.items():
        if key == 'x':
            given['x_bytes'] = e4m3fn_bytes(full / np.repeat(scale.astype(np.float64), 128, axis=1))
            given['x_scale'] = scale
        else:
            given[key] = value
    return given


def reference(x_bytes, x_scale, g, v, m, p, a_words, a_scales, b_words, b_scales):
    return core(e4m3fn_values(x_bytes) * np.repeat(x_scale.astype(np.float64), 128, axis=1), g, v, m, p, a_words, a_scales, b_words, b_scales)

@@ -1,0 +1,452 @@
+from contextlib import ExitStack
+
+import concourse.mybir as mybir
+from concourse.masks import make_identity
+
+N, D, F, R = 2048, 1024, 1024, 256
+SCALE = 2.0
+FLOPS = 2 * N * D * F + 4 * D * F * R
+
+F32 = mybir.dt.float32
+BF16 = mybir.dt.bfloat16
+I32 = mybir.dt.int32
+U32 = mybir.dt.uint32
+U8 = mybir.dt.uint8
+FP8 = mybir.dt.float8_e4m3fn
+FP8X4 = mybir.dt.float8_e4m3fn_x4
+FP4X4 = mybir.dt.float4_e2m1fn_x4
+ALU = mybir.AluOpType
+ACT = mybir.ActivationFunctionType
+
+P = 128
+PACK = 4
+KP = P * PACK
+N_PASSES = N // KP
+TILES = F // P
+
+
+def tile_columnnormbackwardtwoproducts_kernel(
+    tc, x_bytes, x_scale, g, v, m, p, a_words, a_scales, b_words, b_scales, out_0, out_1
+):
+    nc = tc.nc
+    with ExitStack() as ctx:
+        keep = ctx.enter_context(tc.tile_pool(name="keep", bufs=1))
+        ring = ctx.enter_context(tc.tile_pool(name="ring", bufs=3))
+        grad_ps = ctx.enter_context(tc.psum_pool(name="grad_ps", bufs=1))
+        misc_ps = ctx.enter_context(tc.psum_pool(name="misc_ps", bufs=4))
+        ctx.enter_context(tc.manual_schedule())
+
+        def kept(name, shape, dtype):
+            return keep.tile(shape, dtype, name=name, align_bytes=64)
+
+        xs = kept("xs", [P, N_PASSES, PACK * 8], F32)
+        xb = [kept("x_byte_tile%d" % j, [P, PACK, D], U8) for j in range(N_PASSES)]
+        g_raw = {(fg, j): kept("g_raw%d_%d" % (fg, j), [P, PACK, KP], BF16) for fg in range(2) for j in range(N_PASSES)}
+        v_sb = [kept("v_sb%d" % fg, [P, D // P, KP], BF16) for fg in range(2)]
+        m_sb = kept("m_sb", [P, 2, PACK], BF16)
+        p_row = kept("p_row", [P, D], BF16)
+        a_w = kept("a_w", [P, 2, 2 * R], U8)
+        b_w = kept("b_w", [P, 2, 2 * R], U8)
+        a_s = kept("a_s", [P, 2, R], U8)
+        b_s = kept("b_s", [P, 2, R], U8)
+        ident_bf = kept("ident_bf", [P, P], BF16)
+        ident_f32 = kept("ident_f32", [P, P], F32)
+        x_codes = {(j, h): kept("x_codes%d_%d" % (j, h), [P, KP], U32) for j in range(N_PASSES) for h in range(2)}
+        x_sc = {(j, h): kept("x_sc%d_%d" % (j, h), [P, KP], U8) for j in range(N_PASSES) for h in range(2)}
+        g_codes = {(fg, j): kept("g_codes%d_%d" % (fg, j), [P, KP], U32) for fg in range(2) for j in range(N_PASSES)}
+        g_sc = {(fg, j): kept("g_sc%d_%d" % (fg, j), [P, KP], U8) for fg in range(2) for j in range(N_PASSES)}
+        vt = [kept("vt%d" % i, [P, D], BF16) for i in range(TILES)]
+        c2 = kept("c2", [P, TILES], F32)
+        root = kept("root", [P, TILES], F32)
+        r0 = kept("r0", [P, TILES], F32)
+        nh = kept("nh", [P, TILES], F32)
+        nq = kept("nq", [P, TILES], F32)
+        alpha = kept("alpha", [P, TILES], F32)
+        alpha_m = kept("alpha_m", [P, TILES], F32)
+        inv_c2 = kept("inv_c2", [P, TILES], F32)
+        dots = kept("dots", [P, 2 * TILES], F32)
+        neg_proj = kept("neg_proj", [P, TILES], F32)
+        diag_junk = kept("diag_junk", [P, PACK, P], F32)
+        up_codes = {(fg, dg): kept("up_codes%d_%d" % (fg, dg), [P, KP], U32) for fg in range(2) for dg in range(2)}
+        up_sc = {(fg, dg): kept("up_sc%d_%d" % (fg, dg), [P, KP], U8) for fg in range(2) for dg in range(2)}
+        dv_planes = [kept("dv_planes%d" % fg, [P, PACK, D], BF16) for fg in range(2)]
+        dv_codes = {(fg, c): kept("dv_codes%d_%d" % (fg, c), [P, 256], U32) for fg in range(2) for c in range(4)}
+        dv_sc = {(fg, c): kept("dv_sc%d_%d" % (fg, c), [P, 256], U8) for fg in range(2) for c in range(4)}
+        live = {}
+
+        def load_x(j, cols):
+            rows = x_bytes[j * KP : (j + 1) * KP, :].rearrange("(p t) d -> p t d", t=PACK)
+            nc.sync.dma_start(out=xb[j][:, :, cols], in_=rows[:, :, cols])
+
+        def load_g(fg, j):
+            rows = g[j * KP : (j + 1) * KP, fg * KP : (fg + 1) * KP]
+            nc.sync.dma_start(out=g_raw[fg, j][:], in_=rows.rearrange("(p t) f -> p t f", t=PACK))
+
+        def load_v(fg):
+            cols = v[:, fg * KP : (fg + 1) * KP]
+            nc.sync.dma_start(out=v_sb[fg][:], in_=cols.rearrange("(c p) f -> p c f", p=P))
+
+        def load_weight(words, scales, w_sb, s_sb):
+            nc.sync.dma_start(out=w_sb[:].bitcast(I32), in_=words.rearrange("g p n -> p g n").bitcast(I32))
+            for q in range(4):
+                nc.sync.dma_start(
+                    out=s_sb[32 * q : 32 * q + 4, :, :].bitcast(I32),
+                    in_=scales[:, 4 * q : 4 * q + 4, :].rearrange("g q n -> q g n").bitcast(I32),
+                )
+
+        def copy_on(engine, out, in_):
+            if engine == "vector":
+                nc.vector.tensor_copy(out=out, in_=in_)
+            else:
+                nc.scalar.copy(out=out, in_=in_)
+
+        def widen(j, h):
+            wide = ring.tile([P, PACK, KP], BF16, name="x_wide", align_bytes=64)
+            for t in range(PACK):
+                for b in range(4):
+                    blk = 4 * h + b
+                    nc.scalar.activation(
+                        out=wide[:, t, b * P : (b + 1) * P],
+                        in_=xb[j][:, t, blk * P : (blk + 1) * P].bitcast(FP8),
+                        func=ACT.Copy,
+                        scale=xs[:, j, 8 * t + blk : 8 * t + blk + 1],
+                    )
+            live["x_wide", j, h] = wide
+
+        def weave_x(j, h):
+            woven = ring.tile([P, KP, PACK], BF16, name="woven", align_bytes=64)
+            nc.vector.tensor_copy(out=woven[:], in_=live["x_wide", j, h][:].rearrange("p t c -> p c t"))
+            live["x_woven", j, h] = woven
+
+        def quant_x(j, h):
+            nc.vector.quantize_mx(
+                out=x_codes[j, h][:].bitcast(FP8X4),
+                scales=x_sc[j, h][:],
+                in_=live["x_woven", j, h][:].rearrange("p c t -> p (c t)"),
+            )
+
+        def weave_g(fg, j, engine):
+            woven = ring.tile([P, KP, PACK], BF16, name="woven", align_bytes=64)
+            copy_on(
+                engine,
+                woven[:].rearrange("p (s m) t -> p m s t", s=PACK),
+                g_raw[fg, j][:].rearrange("p t (m s) -> p m s t", s=PACK),
+            )
+            live["g_woven", fg, j] = woven
+
+        def quant_g(fg, j):
+            nc.vector.quantize_mx(
+                out=g_codes[fg, j][:].bitcast(FP8X4),
+                scales=g_sc[fg, j][:],
+                in_=live["g_woven", fg, j][:].rearrange("p c t -> p (c t)"),
+            )
+
+        def turn_v(i):
+            fg, s = divmod(i, PACK)
+            bank = misc_ps.tile([P, D], BF16, name="misc")
+            for c in range(D // P):
+                nc.tensor.transpose(bank[:, c * P : (c + 1) * P], v_sb[fg][:, c, s:KP:PACK], ident_bf[:])
+            live["vt_bank", i] = bank
+
+        def fetch_vt(i):
+            nc.scalar.copy(out=vt[i][:], in_=live["vt_bank", i][:])
+
+        def gram(fg):
+            bank = misc_ps.tile([P, PACK, P], F32, name="misc")
+            for s in range(PACK):
+                for c in range(D // P):
+                    cols = v_sb[fg][:, c, s:KP:PACK]
+                    nc.tensor.matmul(bank[:, s, :], lhsT=cols, rhs=cols, start=(c == 0), stop=(c == D // P - 1))
+            live["gram", fg] = bank
+
+        def gram_diagonal(fg):
+            for s in range(PACK):
+                i = PACK * fg + s
+                nc.vector.scalar_tensor_tensor(
+                    out=diag_junk[:, s, :], in0=live["gram", fg][:, s, :], scalar=1.0, in1=ident_bf[:],
+                    op0=ALU.mult, op1=ALU.mult, accum_out=c2[:, i : i + 1],
+                )
+
+        def grad_pass(i, j):
+            fg, s = divmod(i, PACK)
+            for h in range(2):
+                if j == 0:
+                    live["grad", i, h] = grad_ps.tile([P, KP], F32, name="grad%d_%d" % (i % 2, h))
+                nc.tensor.matmul_mx(
+                    out=live["grad", i, h][:],
+                    lhsT=g_codes[fg, j][:, s * P : (s + 1) * P].bitcast(FP8X4),
+                    lhsT_scale=g_sc[fg, j][:, s * P : (s + 1) * P],
+                    rhs=x_codes[j, h][:].bitcast(FP8X4),
+                    rhs_scale=x_sc[j, h][:],
+                    start=(j == 0),
+                    stop=(j == N_PASSES - 1),
+                )
+
+        def dot(i):
+            resid = ring.tile([P, D], F32, name="resid", align_bytes=64)
+            live["resid", i] = resid
+            for h in range(2):
+                cols = slice(h * KP, (h + 1) * KP)
+                nc.vector.scalar_tensor_tensor(
+                    out=resid[:, cols], in0=live["grad", i, h][:], scalar=-1.0, in1=vt[i][:, cols],
+                    op0=ALU.mult, op1=ALU.mult, accum_out=dots[:, 2 * i + h : 2 * i + h + 1],
+                )
+
+        def projection(i):
+            nc.vector.tensor_scalar(
+                out=neg_proj[:, i : i + 1], in0=dots[:, 2 * i : 2 * i + 1], scalar1=dots[:, 2 * i + 1 : 2 * i + 2],
+                scalar2=inv_c2[:, i : i + 1], op0=ALU.add, op1=ALU.mult,
+            )
+
+        def residual(i):
+            for h in range(2):
+                cols = slice(h * KP, (h + 1) * KP)
+                nc.vector.scalar_tensor_tensor(
+                    out=live["resid", i][:, cols], in0=vt[i][:, cols], scalar=neg_proj[:, i : i + 1],
+                    in1=live["grad", i, h][:], op0=ALU.mult, op1=ALU.add,
+                )
+
+        def make_up(i):
+            up_t = ring.tile([P, D], BF16, name="up_t", align_bytes=64)
+            nc.vector.scalar_tensor_tensor(
+                out=up_t[:], in0=live["resid", i][:], scalar=alpha[:, i : i + 1], in1=p_row[:],
+                op0=ALU.mult, op1=ALU.mult,
+            )
+            live["up_t", i] = up_t
+
+        def turn_up(i):
+            words = live["up_t", i][:].bitcast(F32)
+            bank = misc_ps.tile([P, PACK, P], F32, name="misc")
+            for dg in range(2):
+                for u in range(2):
+                    nc.tensor.transpose(bank[:, 2 * dg + u, :], words[:, 256 * dg + u : 256 * (dg + 1) : 2], ident_f32[:])
+            live["up_bank", i] = bank
+
+        def fetch_up(i):
+            woven = ring.tile([P, 2, KP], BF16, name="up_woven", align_bytes=64)
+            nc.scalar.copy(
+                out=woven[:].bitcast(F32).rearrange("p g (f u) -> p g f u", u=2),
+                in_=live["up_bank", i][:].rearrange("p (g u) f -> p g f u", u=2),
+            )
+            live["up_woven", i] = woven
+
+        def quant_up(i):
+            fg, s = divmod(i, PACK)
+            for dg in range(2):
+                nc.vector.quantize_mx(
+                    out=up_codes[fg, dg][:, s * P : (s + 1) * P].bitcast(FP8X4),
+                    scales=up_sc[fg, dg][:, s * P : (s + 1) * P],
+                    in_=live["up_woven", i][:, dg, :],
+                )
+
+        def make_dv(i, cols):
+            fg, s = divmod(i, PACK)
+            nc.scalar.activation(
+                out=dv_planes[fg][:, s, cols], in_=live["resid", i][:, cols], func=ACT.Copy, scale=alpha_m[:, i : i + 1]
+            )
+
+        def weave_dv(fg, c, engine):
+            woven = ring.tile([P, 256, PACK], BF16, name="dv_woven", align_bytes=64)
+            copy_on(engine, woven[:], dv_planes[fg][:, :, 256 * c : 256 * (c + 1)].rearrange("p t c -> p c t"))
+            live["dv_woven", fg, c] = woven
+
+        def quant_dv(fg, c):
+            nc.vector.quantize_mx(
+                out=dv_codes[fg, c][:].bitcast(FP8X4),
+                scales=dv_sc[fg, c][:],
+                in_=live["dv_woven", fg, c][:].rearrange("p c t -> p (c t)"),
+            )
+
+        def db_product(fg):
+            for rh in range(2):
+                bank = misc_ps.tile([P, KP], F32, name="misc")
+                for dg in range(2):
+                    nc.tensor.matmul_mx(
+                        out=bank[:],
+                        lhsT=a_w[:, dg, 2 * P * rh : 2 * P * (rh + 1)].bitcast(FP4X4),
+                        lhsT_scale=a_s[:, dg, P * rh : P * (rh + 1)],
+                        rhs=up_codes[fg, dg][:].bitcast(FP8X4),
+                        rhs_scale=up_sc[fg, dg][:],
+                        start=(dg == 0),
+                        stop=(dg == 1),
+                    )
+                live["db", fg, rh] = bank
+
+        def db_store(fg):
+            for rh in range(2):
+                res = ring.tile([P, P, PACK], F32, name="result", bufs=8, align_bytes=64)
+                nc.scalar.activation(
+                    out=res[:], in_=live["db", fg, rh][:].rearrange("p (s m) -> p m s", s=PACK), func=ACT.Copy, scale=SCALE
+                )
+                nc.sync.dma_start(
+                    out=out_1[rh * P : (rh + 1) * P, fg * KP : (fg + 1) * KP], in_=res[:].rearrange("p m s -> p (m s)")
+                )
+
+        def da_product(c):
+            bank = grad_ps.tile([P, 2, R], F32, name="grad%d_%d" % (c // 2, c % 2))
+            for e in range(2):
+                for rh in range(2):
+                    for fg in range(2):
+                        nc.tensor.matmul_mx(
+                            out=bank[:, e, P * rh : P * (rh + 1)],
+                            lhsT=dv_codes[fg, c][:, e * P : (e + 1) * P].bitcast(FP8X4),
+                            lhsT_scale=dv_sc[fg, c][:, e * P : (e + 1) * P],
+                            rhs=b_w[:, fg, 2 * P * rh : 2 * P * (rh + 1)].bitcast(FP4X4),
+                            rhs_scale=b_s[:, fg, P * rh : P * (rh + 1)],
+                            start=(fg == 0),
+                            stop=(fg == 1),
+                        )
+            live["da", c] = bank
+
+        def da_store(c):
+            res = ring.tile([P, 2, R], F32, name="result", bufs=8, align_bytes=64)
+            nc.scalar.activation(out=res[:], in_=live["da", c][:], func=ACT.Copy, scale=SCALE)
+            nc.sync.dma_start(out=out_0[256 * c : 256 * (c + 1), :].rearrange("(e p) r -> p e r", p=P), in_=res[:])
+
+        nc.sync.dma_start(out=xs[:], in_=x_scale.rearrange("(j p t) b -> p j (t b)", p=P, t=PACK))
+        load_x(0, slice(0, KP))
+        load_g(0, 0)
+        load_x(0, slice(KP, D))
+        load_g(0, 1)
+        load_x(1, slice(0, D))
+        load_v(0)
+        load_g(0, 2)
+        load_x(2, slice(0, D))
+        load_v(1)
+        load_g(0, 3)
+        load_x(3, slice(0, D))
+        make_identity(nc, ident_bf[:])
+        make_identity(nc, ident_f32[:])
+        nc.gpsimd.memset(a_s[:].bitcast(I32), 0)
+        nc.gpsimd.memset(b_s[:].bitcast(I32), 0)
+        nc.sync.dma_start(out=m_sb[:], in_=m.rearrange("(g p s) -> p g s", p=P, s=PACK))
+        for j in range(N_PASSES):
+            load_g(1, j)
+        nc.sync.dma_start(out=p_row[:], in_=p.partition_broadcast(P))
+        load_weight(a_words, a_scales, a_w, a_s)
+        load_weight(b_words, b_scales, b_w, b_s)
+
+        weave_g(0, 0, "vector")
+        widen(0, 0)
+        weave_x(0, 0)
+        quant_g(0, 0)
+        quant_x(0, 0)
+        widen(0, 1)
+        weave_x(0, 1)
+        weave_g(0, 1, "vector")
+        quant_x(0, 1)
+        quant_g(0, 1)
+        turn_v(0)
+        turn_v(1)
+        gram(0)
+        grad_pass(0, 0)
+        grad_pass(1, 0)
+        widen(1, 0)
+        fetch_vt(0)
+        fetch_vt(1)
+        weave_x(1, 0)
+        weave_g(0, 2, "vector")
+        quant_x(1, 0)
+        quant_g(0, 2)
+        widen(1, 1)
+        gram_diagonal(0)
+        weave_x(1, 1)
+        weave_g(0, 3, "vector")
+        quant_x(1, 1)
+        quant_g(0, 3)
+        gram(1)
+        turn_v(2)
+        turn_v(3)
+        grad_pass(0, 1)
+        grad_pass(1, 1)
+        widen(2, 0)
+        weave_x(2, 0)
+        gram_diagonal(1)
+        quant_x(2, 0)
+        widen(2, 1)
+        nc.scalar.activation(out=root[:], in_=c2[:], func=ACT.Sqrt, scale=float(N))
+        nc.vector.reciprocal(out=inv_c2[:], in_=c2[:])
+        weave_x(2, 1)
+        nc.vector.reciprocal(out=r0[:], in_=root[:])
+        quant_x(2, 1)
+        nc.vector.scalar_tensor_tensor(out=nh[:], in0=c2[:], scalar=-0.5 * N, in1=r0[:], op0=ALU.mult, op1=ALU.mult)
+        grad_pass(0, 2)
+        grad_pass(1, 2)
+        widen(3, 0)
+        fetch_vt(2)
+        weave_x(3, 0)
+        nc.vector.tensor_tensor(out=nq[:], in0=nh[:], in1=r0[:], op=ALU.mult)
+        quant_x(3, 0)
+        nc.vector.scalar_tensor_tensor(out=alpha[:], in0=nq[:], scalar=1.5, in1=r0[:], op0=ALU.add, op1=ALU.mult)
+        widen(3, 1)
+        fetch_vt(3)
+        weave_x(3, 1)
+        nc.vector.tensor_tensor(out=alpha_m[:], in0=alpha[:], in1=m_sb[:].rearrange("p g s -> p (g s)"), op=ALU.mult)
+        quant_x(3, 1)
+        grad_pass(0, 3)
+        grad_pass(1, 3)
+        weave_g(1, 0, "vector")
+        quant_g(1, 0)
+
+        for i in range(TILES):
+            last_pass_waits = i == 3
+            if 1 <= i < TILES - 1:
+                for j in range(N_PASSES - 1 if last_pass_waits else N_PASSES):
+                    grad_pass(i + 1, j)
+            if i >= 1:
+                make_dv(i - 1, slice(0, D))
+            if 3 <= i <= 6:
+                fetch_vt(i + 1)
+            dot(i)
+            if i <= 2:
+                weave_g(1, i + 1, "scalar")
+            if i >= 4:
+                weave_dv(0, i - 4, "scalar")
+            if i >= 1:
+                make_up(i - 1)
+                turn_up(i - 1)
+                fetch_up(i - 1)
+            if 2 <= i <= 5:
+                turn_v(i + 2)
+            projection(i)
+            if i >= 2:
+                quant_up(i - 2)
+            if i == 5:
+                db_product(0)
+            if i == 6:
+                db_store(0)
+            if 1 <= i <= 3:
+                quant_g(1, i)
+            if last_pass_waits:
+                grad_pass(i + 1, N_PASSES - 1)
+            if i >= 5:
+                quant_dv(0, i - 5)
+            residual(i)
+
+        last = TILES - 1
+        make_dv(last, slice(0, KP))
+        make_dv(last, slice(KP, D))
+        quant_up(last - 1)
+        quant_dv(0, 3)
+        make_up(last)
+        turn_up(last)
+        fetch_up(last)
+        weave_dv(1, 0, "vector")
+        weave_dv(1, 1, "vector")
+        quant_dv(1, 0)
+        da_product(0)
+        da_store(0)
+        quant_up(last)
+        db_product(1)
+        quant_dv(1, 1)
+        da_product(1)
+        db_store(1)
+        weave_dv(1, 2, "vector")
+        weave_dv(1, 3, "vector")
+        quant_dv(1, 2)
+        da_product(2)
+        quant_dv(1, 3)
+        da_product(3)
+        da_store(1)
+        da_store(2)
+        da_store(3)

@@ -32,15 +32,18 @@ def tile_columnnormbackwardtwoproducts_kernel(
     with ExitStack() as ctx:
         keep = ctx.enter_context(tc.tile_pool(name="keep", bufs=1))
         ring = ctx.enter_context(tc.tile_pool(name="ring", bufs=3))
-        grad_ps = ctx.enter_context(tc.psum_pool(name="grad_ps", bufs=1))
-        misc_ps = ctx.enter_context(tc.psum_pool(name="misc_ps", bufs=4))
+        psum = ctx.enter_context(tc.psum_pool(name="psum", bufs=1))
         ctx.enter_context(tc.manual_schedule())
 
         def kept(name, shape, dtype):
             return keep.tile(shape, dtype, name=name, align_bytes=64)
 
         xs = kept("xs", [P, N_PASSES, PACK * 8], F32)
-        xb = [kept("x_byte_tile%d" % j, [P, PACK, D], U8) for j in range(N_PASSES)]
+        xb = {(0, h): kept("x_byte_half%d" % h, [P, PACK, KP], U8) for h in range(2)}
+        for j in range(1, N_PASSES):
+            whole = kept("x_byte_tile%d" % j, [P, PACK, D], U8)
+            live_x = [whole[:, :, h * KP : (h + 1) * KP] for h in range(2)]
+            xb[j, 0], xb[j, 1], xb[j] = live_x[0], live_x[1], whole
         g_raw = {(fg, j): kept("g_raw%d_%d" % (fg, j), [P, PACK, KP], BF16) for fg in range(2) for j in range(N_PASSES)}
         v_sb = [kept("v_sb%d" % fg, [P, D // P, KP], BF16) for fg in range(2)]
         m_sb = kept("m_sb", [P, 2, PACK], BF16)
@@ -72,11 +75,20 @@ def tile_columnnormbackwardtwoproducts_kernel(
         dv_planes = [kept("dv_planes%d" % fg, [P, PACK, D], BF16) for fg in range(2)]
         dv_codes = {(fg, c): kept("dv_codes%d_%d" % (fg, c), [P, 256], U32) for fg in range(2) for c in range(4)}
         dv_sc = {(fg, c): kept("dv_sc%d_%d" % (fg, c), [P, 256], U8) for fg in range(2) for c in range(4)}
+        n_rows = kept("n_rows", [P, 1], F32)
+        root_n = kept("root_n", [P, 1], F32)
+        root_nc = kept("root_nc", [P, TILES], F32)
         live = {}
 
-        def load_x(j, cols):
+        def bank_tile(b, shape, dtype):
+            return psum.tile(shape, dtype, name="bank%d" % b)
+
+        def load_x(j, h=None):
             rows = x_bytes[j * KP : (j + 1) * KP, :].rearrange("(p t) d -> p t d", t=PACK)
-            nc.sync.dma_start(out=xb[j][:, :, cols], in_=rows[:, :, cols])
+            if h is None:
+                nc.sync.dma_start(out=xb[j][:], in_=rows)
+            else:
+                nc.sync.dma_start(out=xb[j, h][:], in_=rows[:, :, h * KP : (h + 1) * KP])
 
         def load_g(fg, j):
             rows = g[j * KP : (j + 1) * KP, fg * KP : (fg + 1) * KP]
@@ -100,22 +112,30 @@ def tile_columnnormbackwardtwoproducts_kernel(
             else:
                 nc.scalar.copy(out=out, in_=in_)
 
-        def widen(j, h):
-            wide = ring.tile([P, PACK, KP], BF16, name="x_wide", align_bytes=64)
-            for t in range(PACK):
-                for b in range(4):
-                    blk = 4 * h + b
-                    nc.scalar.activation(
-                        out=wide[:, t, b * P : (b + 1) * P],
-                        in_=xb[j][:, t, blk * P : (blk + 1) * P].bitcast(FP8),
-                        func=ACT.Copy,
-                        scale=xs[:, j, 8 * t + blk : 8 * t + blk + 1],
-                    )
-            live["x_wide", j, h] = wide
+        def widen(j, h, first, last, engine):
+            if ("x_wide", j, h) not in live:
+                live["x_wide", j, h] = ring.tile([P, PACK, KP], BF16, name="x_wide", tag="stage", bufs=6, align_bytes=64)
+            for n in range(first, last):
+                t, b = divmod(n, 4)
+                blk = 4 * h + b
+                out = live["x_wide", j, h][:, t, b * P : (b + 1) * P]
+                in_ = xb[j, h][:, t, b * P : (b + 1) * P].bitcast(FP8)
+                scale = xs[:, j, 8 * t + blk : 8 * t + blk + 1]
+                if engine == "vector":
+                    nc.vector.tensor_scalar(out=out, in0=in_, scalar1=scale, scalar2=None, op0=ALU.mult)
+                else:
+                    nc.scalar.activation(out=out, in_=in_, func=ACT.Copy, scale=scale)
 
-        def weave_x(j, h):
-            woven = ring.tile([P, KP, PACK], BF16, name="woven", align_bytes=64)
-            nc.vector.tensor_copy(out=woven[:], in_=live["x_wide", j, h][:].rearrange("p t c -> p c t"))
+        def weave(engine, woven, planes):
+            copy_on(
+                engine,
+                woven.rearrange("p (c i) t -> p c t i", i=4),
+                planes.rearrange("p t (c i) -> p c t i", i=4),
+            )
+
+        def weave_x(j, h, engine):
+            woven = ring.tile([P, KP, PACK], BF16, name="x_woven", tag="stage", bufs=6, align_bytes=64)
+            weave(engine, woven[:], live["x_wide", j, h][:])
             live["x_woven", j, h] = woven
 
         def quant_x(j, h):
@@ -125,25 +145,26 @@ def tile_columnnormbackwardtwoproducts_kernel(
                 in_=live["x_woven", j, h][:].rearrange("p c t -> p (c t)"),
             )
 
-        def weave_g(fg, j, engine):
-            woven = ring.tile([P, KP, PACK], BF16, name="woven", align_bytes=64)
+        def weave_g(fg, j, engine, s0=0, ns=PACK):
+            woven = ring.tile([P, ns * P, PACK], BF16, name="g_woven", bufs=6, align_bytes=64)
             copy_on(
                 engine,
-                woven[:].rearrange("p (s m) t -> p m s t", s=PACK),
-                g_raw[fg, j][:].rearrange("p t (m s) -> p m s t", s=PACK),
+                woven[:].rearrange("p (s m) t -> p m t s", s=ns),
+                g_raw[fg, j][:].rearrange("p t (m s) -> p m t s", s=PACK)[:, :, :, s0 : s0 + ns],
             )
-            live["g_woven", fg, j] = woven
+            live["g_woven", fg, j, s0] = woven
 
-        def quant_g(fg, j):
+        def quant_g(fg, j, s0=0, ns=PACK):
+            cols = slice(s0 * P, (s0 + ns) * P)
             nc.vector.quantize_mx(
-                out=g_codes[fg, j][:].bitcast(FP8X4),
-                scales=g_sc[fg, j][:],
-                in_=live["g_woven", fg, j][:].rearrange("p c t -> p (c t)"),
+                out=g_codes[fg, j][:, cols].bitcast(FP8X4),
+                scales=g_sc[fg, j][:, cols],
+                in_=live["g_woven", fg, j, s0][:].rearrange("p c t -> p (c t)"),
             )
 
-        def turn_v(i):
+        def turn_v(i, b):
             fg, s = divmod(i, PACK)
-            bank = misc_ps.tile([P, D], BF16, name="misc")
+            bank = bank_tile(b, [P, D], BF16)
             for c in range(D // P):
                 nc.tensor.transpose(bank[:, c * P : (c + 1) * P], v_sb[fg][:, c, s:KP:PACK], ident_bf[:])
             live["vt_bank", i] = bank
@@ -151,8 +172,8 @@ def tile_columnnormbackwardtwoproducts_kernel(
         def fetch_vt(i):
             nc.scalar.copy(out=vt[i][:], in_=live["vt_bank", i][:])
 
-        def gram(fg):
-            bank = misc_ps.tile([P, PACK, P], F32, name="misc")
+        def gram(fg, b):
+            bank = bank_tile(b, [P, PACK, P], F32)
             for s in range(PACK):
                 for c in range(D // P):
                     cols = v_sb[fg][:, c, s:KP:PACK]
@@ -171,7 +192,7 @@ def tile_columnnormbackwardtwoproducts_kernel(
             fg, s = divmod(i, PACK)
             for h in range(2):
                 if j == 0:
-                    live["grad", i, h] = grad_ps.tile([P, KP], F32, name="grad%d_%d" % (i % 2, h))
+                    live["grad", i, h] = bank_tile(2 * (i % 3) + h, [P, KP], F32)
                 nc.tensor.matmul_mx(
                     out=live["grad", i, h][:],
                     lhsT=g_codes[fg, j][:, s * P : (s + 1) * P].bitcast(FP8X4),
@@ -198,25 +219,26 @@ def tile_columnnormbackwardtwoproducts_kernel(
                 scalar2=inv_c2[:, i : i + 1], op0=ALU.add, op1=ALU.mult,
             )
 
-        def residual(i):
-            for h in range(2):
-                cols = slice(h * KP, (h + 1) * KP)
-                nc.vector.scalar_tensor_tensor(
-                    out=live["resid", i][:, cols], in0=vt[i][:, cols], scalar=neg_proj[:, i : i + 1],
-                    in1=live["grad", i, h][:], op0=ALU.mult, op1=ALU.add,
-                )
+        def residual(i, h):
+            cols = slice(h * KP, (h + 1) * KP)
+            nc.vector.scalar_tensor_tensor(
+                out=live["resid", i][:, cols], in0=vt[i][:, cols], scalar=neg_proj[:, i : i + 1],
+                in1=live["grad", i, h][:], op0=ALU.mult, op1=ALU.add,
+            )
 
         def make_up(i):
             up_t = ring.tile([P, D], BF16, name="up_t", align_bytes=64)
-            nc.vector.scalar_tensor_tensor(
-                out=up_t[:], in0=live["resid", i][:], scalar=alpha[:, i : i + 1], in1=p_row[:],
-                op0=ALU.mult, op1=ALU.mult,
-            )
+            for h in range(2):
+                cols = slice(h * KP, (h + 1) * KP)
+                nc.vector.scalar_tensor_tensor(
+                    out=up_t[:, cols], in0=live["resid", i][:, cols], scalar=alpha[:, i : i + 1], in1=p_row[:, cols],
+                    op0=ALU.mult, op1=ALU.mult,
+                )
             live["up_t", i] = up_t
 
         def turn_up(i):
             words = live["up_t", i][:].bitcast(F32)
-            bank = misc_ps.tile([P, PACK, P], F32, name="misc")
+            bank = bank_tile(6, [P, PACK, P], F32)
             for dg in range(2):
                 for u in range(2):
                     nc.tensor.transpose(bank[:, 2 * dg + u, :], words[:, 256 * dg + u : 256 * (dg + 1) : 2], ident_f32[:])
@@ -239,15 +261,31 @@ def tile_columnnormbackwardtwoproducts_kernel(
                     in_=live["up_woven", i][:, dg, :],
                 )
 
-        def make_dv(i, cols):
+        def make_dv(i, first, last):
             fg, s = divmod(i, PACK)
+            cols = slice(first, last)
             nc.scalar.activation(
                 out=dv_planes[fg][:, s, cols], in_=live["resid", i][:, cols], func=ACT.Copy, scale=alpha_m[:, i : i + 1]
             )
 
         def weave_dv(fg, c, engine):
-            woven = ring.tile([P, 256, PACK], BF16, name="dv_woven", align_bytes=64)
-            copy_on(engine, woven[:], dv_planes[fg][:, :, 256 * c : 256 * (c + 1)].rearrange("p t c -> p c t"))
+            woven = ring.tile([P, 256, PACK], BF16, name="dv_woven", bufs=4, align_bytes=64)
+            weave(engine, woven[:], dv_planes[fg][:, :, 256 * c : 256 * (c + 1)])
+            live["dv_woven", fg, c] = woven
+
+        def turn_dv(fg, c, b):
+            bank = bank_tile(b, [P, 256 * PACK], BF16)
+            for e in range(2):
+                cols = slice(256 * c + P * e, 256 * c + P * (e + 1))
+                nc.tensor.matmul(
+                    bank[:, e * KP : (e + 1) * KP], lhsT=ident_bf[:],
+                    rhs=dv_planes[fg][:, :, cols].rearrange("p t c -> p c t"), start=True, stop=True,
+                )
+            live["dv_bank", fg, c] = bank
+
+        def fetch_dv(fg, c):
+            woven = ring.tile([P, 256, PACK], BF16, name="dv_woven", bufs=4, align_bytes=64)
+            nc.scalar.copy(out=woven[:].rearrange("p c t -> p (c t)"), in_=live["dv_bank", fg, c][:])
             live["dv_woven", fg, c] = woven
 
         def quant_dv(fg, c):
@@ -257,9 +295,9 @@ def tile_columnnormbackwardtwoproducts_kernel(
                 in_=live["dv_woven", fg, c][:].rearrange("p c t -> p (c t)"),
             )
 
-        def db_product(fg):
+        def db_product(fg, b):
             for rh in range(2):
-                bank = misc_ps.tile([P, KP], F32, name="misc")
+                bank = bank_tile(b + rh, [P, KP], F32)
                 for dg in range(2):
                     nc.tensor.matmul_mx(
                         out=bank[:],
@@ -272,18 +310,21 @@ def tile_columnnormbackwardtwoproducts_kernel(
                     )
                 live["db", fg, rh] = bank
 
-        def db_store(fg):
-            for rh in range(2):
-                res = ring.tile([P, P, PACK], F32, name="result", bufs=8, align_bytes=64)
-                nc.scalar.activation(
-                    out=res[:], in_=live["db", fg, rh][:].rearrange("p (s m) -> p m s", s=PACK), func=ACT.Copy, scale=SCALE
-                )
-                nc.sync.dma_start(
-                    out=out_1[rh * P : (rh + 1) * P, fg * KP : (fg + 1) * KP], in_=res[:].rearrange("p m s -> p (m s)")
-                )
+        def scale_out(engine, out, in_):
+            if engine == "vector":
+                nc.vector.tensor_scalar(out=out, in0=in_, scalar1=SCALE, scalar2=None, op0=ALU.mult)
+            else:
+                nc.scalar.activation(out=out, in_=in_, func=ACT.Copy, scale=SCALE)
+
+        def db_store(fg, rh, engine):
+            res = ring.tile([P, P, PACK], F32, name="result", tag="stage", bufs=6, align_bytes=64)
+            scale_out(engine, res[:], live["db", fg, rh][:].rearrange("p (s m) -> p m s", s=PACK))
+            nc.sync.dma_start(
+                out=out_1[rh * P : (rh + 1) * P, fg * KP : (fg + 1) * KP], in_=res[:].rearrange("p m s -> p (m s)")
+            )
 
         def da_product(c):
-            bank = grad_ps.tile([P, 2, R], F32, name="grad%d_%d" % (c // 2, c % 2))
+            bank = bank_tile(c, [P, 2, R], F32)
             for e in range(2):
                 for rh in range(2):
                     for fg in range(2):
@@ -298,155 +339,280 @@ def tile_columnnormbackwardtwoproducts_kernel(
                         )
             live["da", c] = bank
 
-        def da_store(c):
-            res = ring.tile([P, 2, R], F32, name="result", bufs=8, align_bytes=64)
-            nc.scalar.activation(out=res[:], in_=live["da", c][:], func=ACT.Copy, scale=SCALE)
+        def da_store(c, engine):
+            res = ring.tile([P, 2, R], F32, name="result", tag="stage", bufs=6, align_bytes=64)
+            scale_out(engine, res[:], live["da", c][:])
             nc.sync.dma_start(out=out_0[256 * c : 256 * (c + 1), :].rearrange("(e p) r -> p e r", p=P), in_=res[:])
 
-        nc.sync.dma_start(out=xs[:], in_=x_scale.rearrange("(j p t) b -> p j (t b)", p=P, t=PACK))
-        load_x(0, slice(0, KP))
-        load_g(0, 0)
-        load_x(0, slice(KP, D))
-        load_g(0, 1)
-        load_x(1, slice(0, D))
-        load_v(0)
-        load_g(0, 2)
-        load_x(2, slice(0, D))
-        load_v(1)
-        load_g(0, 3)
-        load_x(3, slice(0, D))
+        def load_small(k):
+            if k == 0:
+                nc.sync.dma_start(out=xs[:], in_=x_scale.rearrange("(j p t) b -> p j (t b)", p=P, t=PACK))
+            if k == 1:
+                nc.sync.dma_start(out=m_sb[:], in_=m.rearrange("(g p s) -> p g s", p=P, s=PACK))
+            if k == 2:
+                nc.sync.dma_start(out=p_row[:], in_=p.partition_broadcast(P))
+            if k == 3:
+                load_weight(a_words, a_scales, a_w, a_s)
+                load_weight(b_words, b_scales, b_w, b_s)
+
+        def norm(k):
+            if k == 0:
+                nc.scalar.activation(out=root[:], in_=c2[:], func=ACT.Sqrt)
+            if k == 1:
+                nc.scalar.activation(out=root_nc[:], in_=root[:], func=ACT.Copy, scale=root_n[:])
+            if k == 2:
+                nc.vector.reciprocal(out=inv_c2[:], in_=c2[:])
+            if k == 3:
+                nc.vector.reciprocal(out=r0[:], in_=root_nc[:])
+            if k == 4:
+                nc.vector.scalar_tensor_tensor(out=nh[:], in0=c2[:], scalar=-0.5 * N, in1=r0[:], op0=ALU.mult, op1=ALU.mult)
+            if k == 5:
+                nc.vector.tensor_tensor(out=nq[:], in0=nh[:], in1=r0[:], op=ALU.mult)
+            if k == 6:
+                nc.vector.scalar_tensor_tensor(out=alpha[:], in0=nq[:], scalar=1.5, in1=r0[:], op0=ALU.add, op1=ALU.mult)
+            if k == 7:
+                nc.vector.tensor_tensor(out=alpha_m[:], in0=alpha[:], in1=m_sb[:].rearrange("p g s -> p (g s)"), op=ALU.mult)
+
+        nc.vector.memset(n_rows[:], float(N))
+        nc.scalar.activation(out=root_n[:], in_=n_rows[:], func=ACT.Sqrt)
         make_identity(nc, ident_bf[:])
         make_identity(nc, ident_f32[:])
         nc.gpsimd.memset(a_s[:].bitcast(I32), 0)
         nc.gpsimd.memset(b_s[:].bitcast(I32), 0)
-        nc.sync.dma_start(out=m_sb[:], in_=m.rearrange("(g p s) -> p g s", p=P, s=PACK))
+        load_small(0)
+        load_x(0, 0)
+        load_g(0, 0)
+        load_x(0, 1)
+        load_x(1)
+        load_v(0)
+        load_g(0, 1)
+        load_x(2)
+        load_g(0, 2)
+        load_v(1)
+        load_x(3)
+        load_g(0, 3)
+        load_small(1)
         for j in range(N_PASSES):
             load_g(1, j)
-        nc.sync.dma_start(out=p_row[:], in_=p.partition_broadcast(P))
-        load_weight(a_words, a_scales, a_w, a_s)
-        load_weight(b_words, b_scales, b_w, b_s)
-
-        weave_g(0, 0, "vector")
-        widen(0, 0)
-        weave_x(0, 0)
-        quant_g(0, 0)
+        load_small(2)
+        load_small(3)
+        widen(0, 0, 8, 16, "vector")
+        turn_v(1, 7)
+        weave_g(0, 0, "vector", 0, 2)
+        widen(0, 0, 0, 8, "scalar")
+        weave_x(0, 0, "vector")
+        widen(0, 1, 0, 16, "scalar")
         quant_x(0, 0)
-        widen(0, 1)
-        weave_x(0, 1)
-        weave_g(0, 1, "vector")
+        quant_g(0, 0, 0, 2)
+        weave_x(0, 1, "vector")
+        widen(1, 0, 0, 16, "scalar")
+        weave_g(0, 1, "vector", 0, 2)
         quant_x(0, 1)
-        quant_g(0, 1)
-        turn_v(0)
-        turn_v(1)
-        gram(0)
-        grad_pass(0, 0)
-        grad_pass(1, 0)
-        widen(1, 0)
-        fetch_vt(0)
-        fetch_vt(1)
-        weave_x(1, 0)
-        weave_g(0, 2, "vector")
+        weave_x(1, 0, "vector")
+        quant_g(0, 1, 0, 2)
+        widen(1, 1, 0, 16, "scalar")
         quant_x(1, 0)
-        quant_g(0, 2)
-        widen(1, 1)
-        gram_diagonal(0)
-        weave_x(1, 1)
-        weave_g(0, 3, "vector")
+        weave_x(1, 1, "vector")
+        weave_g(0, 2, "vector", 0, 2)
+        widen(2, 0, 0, 16, "scalar")
+        grad_pass(1, 0)
         quant_x(1, 1)
-        quant_g(0, 3)
-        gram(1)
-        turn_v(2)
-        turn_v(3)
-        grad_pass(0, 1)
-        grad_pass(1, 1)
-        widen(2, 0)
-        weave_x(2, 0)
-        gram_diagonal(1)
+        weave_x(2, 0, "vector")
+        widen(2, 1, 0, 16, "scalar")
+        weave_g(0, 3, "vector", 0, 2)
+        gram(0, 4)
+        gram_diagonal(0)
+        weave_x(2, 1, "vector")
         quant_x(2, 0)
-        widen(2, 1)
-        nc.scalar.activation(out=root[:], in_=c2[:], func=ACT.Sqrt, scale=float(N))
-        nc.vector.reciprocal(out=inv_c2[:], in_=c2[:])
-        weave_x(2, 1)
-        nc.vector.reciprocal(out=r0[:], in_=root[:])
+        gram(1, 5)
+        turn_v(0, 6)
         quant_x(2, 1)
-        nc.vector.scalar_tensor_tensor(out=nh[:], in0=c2[:], scalar=-0.5 * N, in1=r0[:], op0=ALU.mult, op1=ALU.mult)
-        grad_pass(0, 2)
-        grad_pass(1, 2)
-        widen(3, 0)
-        fetch_vt(2)
-        weave_x(3, 0)
-        nc.vector.tensor_tensor(out=nq[:], in0=nh[:], in1=r0[:], op=ALU.mult)
+        grad_pass(0, 0)
+        quant_g(0, 3, 0, 2)
+        widen(3, 0, 0, 16, "scalar")
+        quant_g(0, 2, 0, 2)
+        gram_diagonal(1)
+        weave_x(3, 0, "vector")
+        widen(3, 1, 0, 16, "scalar")
+        weave_x(3, 1, "vector")
+        fetch_vt(1)
+        grad_pass(0, 1)
+        turn_v(3, 7)
+        weave_g(0, 0, "scalar", 2, 2)
         quant_x(3, 0)
-        nc.vector.scalar_tensor_tensor(out=alpha[:], in0=nq[:], scalar=1.5, in1=r0[:], op0=ALU.add, op1=ALU.mult)
-        widen(3, 1)
-        fetch_vt(3)
-        weave_x(3, 1)
-        nc.vector.tensor_tensor(out=alpha_m[:], in0=alpha[:], in1=m_sb[:].rearrange("p g s -> p (g s)"), op=ALU.mult)
+        norm(0)
+        grad_pass(0, 2)
         quant_x(3, 1)
+        weave_g(0, 1, "scalar", 2, 2)
         grad_pass(0, 3)
+        norm(1)
+        grad_pass(1, 1)
+        quant_g(0, 0, 2, 2)
+        grad_pass(1, 2)
+        norm(3)
+        norm(2)
+        fetch_vt(0)
+        quant_g(0, 1, 2, 2)
+        weave_g(0, 2, "scalar", 2, 2)
         grad_pass(1, 3)
-        weave_g(1, 0, "vector")
-        quant_g(1, 0)
-
-        for i in range(TILES):
-            last_pass_waits = i == 3
-            if 1 <= i < TILES - 1:
-                for j in range(N_PASSES - 1 if last_pass_waits else N_PASSES):
-                    grad_pass(i + 1, j)
-            if i >= 1:
-                make_dv(i - 1, slice(0, D))
-            if 3 <= i <= 6:
-                fetch_vt(i + 1)
-            dot(i)
-            if i <= 2:
-                weave_g(1, i + 1, "scalar")
-            if i >= 4:
-                weave_dv(0, i - 4, "scalar")
-            if i >= 1:
-                make_up(i - 1)
-                turn_up(i - 1)
-                fetch_up(i - 1)
-            if 2 <= i <= 5:
-                turn_v(i + 2)
-            projection(i)
-            if i >= 2:
-                quant_up(i - 2)
-            if i == 5:
-                db_product(0)
-            if i == 6:
-                db_store(0)
-            if 1 <= i <= 3:
-                quant_g(1, i)
-            if last_pass_waits:
-                grad_pass(i + 1, N_PASSES - 1)
-            if i >= 5:
-                quant_dv(0, i - 5)
-            residual(i)
-
-        last = TILES - 1
-        make_dv(last, slice(0, KP))
-        make_dv(last, slice(KP, D))
-        quant_up(last - 1)
+        norm(4)
+        dot(0)
+        weave_g(0, 3, "scalar", 2, 2)
+        weave_g(1, 0, "scalar", 0, 2)
+        weave_g(1, 1, "scalar", 0, 2)
+        turn_v(2, 6)
+        norm(5)
+        weave_g(1, 2, "scalar", 0, 2)
+        grad_pass(2, 0)
+        quant_g(0, 2, 2, 2)
+        projection(0)
+        dot(1)
+        fetch_vt(3)
+        fetch_vt(2)
+        residual(0, 0)
+        projection(1)
+        residual(0, 1)
+        grad_pass(2, 1)
+        quant_g(0, 3, 2, 2)
+        residual(1, 0)
+        grad_pass(2, 2)
+        norm(6)
+        grad_pass(2, 3)
+        grad_pass(3, 0)
+        weave_g(1, 3, "scalar", 0, 2)
+        quant_g(1, 0, 0, 2)
+        quant_g(1, 1, 0, 2)
+        norm(7)
+        turn_v(4, 7)
+        make_up(0)
+        residual(1, 1)
+        dot(2)
+        fetch_vt(4)
+        make_up(1)
+        grad_pass(3, 1)
+        grad_pass(3, 2)
+        projection(2)
+        make_dv(0, 0, 1024)
+        weave_g(1, 0, "scalar", 2, 2)
+        make_dv(1, 0, 1024)
+        grad_pass(3, 3)
+        weave_g(1, 1, "scalar", 2, 2)
+        dot(3)
+        grad_pass(4, 0)
+        turn_up(0)
+        grad_pass(4, 1)
+        turn_v(5, 7)
+        residual(2, 0)
+        projection(3)
+        quant_g(1, 2, 0, 2)
+        residual(2, 1)
+        grad_pass(5, 0)
+        grad_pass(5, 1)
+        make_up(2)
+        fetch_up(0)
+        residual(3, 0)
+        quant_g(1, 3, 0, 2)
+        residual(3, 1)
+        fetch_vt(5)
+        weave_g(1, 2, "scalar", 2, 2)
+        weave_g(1, 3, "scalar", 2, 2)
+        grad_pass(4, 2)
+        grad_pass(5, 2)
+        grad_pass(4, 3)
+        grad_pass(5, 3)
+        make_dv(2, 0, 1024)
+        make_up(3)
+        quant_g(1, 2, 2, 2)
+        make_dv(3, 0, 1024)
+        turn_v(6, 7)
+        quant_g(1, 0, 2, 2)
+        turn_up(1)
+        grad_pass(6, 0)
+        fetch_up(1)
+        quant_g(1, 1, 2, 2)
+        dot(4)
+        dot(5)
+        quant_g(1, 3, 2, 2)
+        fetch_vt(6)
+        weave_dv(0, 0, "scalar")
+        grad_pass(6, 1)
+        grad_pass(6, 2)
+        projection(4)
+        turn_up(2)
+        weave_dv(0, 1, "scalar")
+        quant_up(1)
+        quant_up(0)
+        projection(5)
+        residual(4, 1)
+        residual(4, 0)
+        make_dv(4, 0, 1024)
+        fetch_up(2)
+        turn_v(7, 7)
+        grad_pass(6, 3)
+        fetch_vt(7)
+        grad_pass(7, 0)
+        grad_pass(7, 1)
+        residual(5, 1)
+        turn_up(3)
+        make_up(4)
+        grad_pass(7, 2)
+        grad_pass(7, 3)
+        residual(5, 0)
+        make_dv(5, 0, 1024)
+        quant_dv(0, 1)
+        fetch_up(3)
+        dot(6)
+        make_up(5)
+        quant_dv(0, 0)
+        dot(7)
+        weave_dv(0, 2, "scalar")
+        projection(6)
+        quant_up(2)
+        turn_up(4)
+        fetch_up(4)
+        quant_up(3)
+        residual(6, 0)
+        residual(6, 1)
+        weave_dv(0, 3, "scalar")
+        turn_up(5)
+        projection(7)
         quant_dv(0, 3)
-        make_up(last)
-        turn_up(last)
-        fetch_up(last)
+        make_up(6)
+        fetch_up(5)
+        residual(7, 0)
+        make_dv(6, 0, 1024)
+        turn_up(6)
+        make_dv(7, 0, 512)
+        fetch_up(6)
+        db_product(0, 4)
+        residual(7, 1)
+        make_up(7)
         weave_dv(1, 0, "vector")
+        turn_up(7)
         weave_dv(1, 1, "vector")
         quant_dv(1, 0)
         da_product(0)
-        da_store(0)
-        quant_up(last)
-        db_product(1)
+        make_dv(7, 512, 1024)
+        db_store(0, 0, "scalar")
+        quant_dv(0, 2)
         quant_dv(1, 1)
         da_product(1)
-        db_store(1)
         weave_dv(1, 2, "vector")
-        weave_dv(1, 3, "vector")
+        quant_up(4)
+        db_store(0, 1, "scalar")
+        quant_up(6)
         quant_dv(1, 2)
-        da_product(2)
+        quant_up(5)
+        weave_dv(1, 3, "scalar")
+        fetch_up(7)
         quant_dv(1, 3)
+        da_product(2)
         da_product(3)
-        da_store(1)
-        da_store(2)
-        da_store(3)
+        quant_up(7)
+        da_store(0, "scalar")
+        da_store(1, "vector")
+        da_store(2, "scalar")
+        da_store(3, "vector")
+        db_product(1, 6)
+        db_store(1, 0, "scalar")
+        db_store(1, 1, "vector")

from contextlib import ExitStack

import concourse.mybir as mybir
from concourse.masks import make_identity

N, D, F, R = 2048, 1024, 1024, 256
SCALE = 2.0
FLOPS = 2 * N * D * F + 4 * D * F * R

F32 = mybir.dt.float32
BF16 = mybir.dt.bfloat16
I32 = mybir.dt.int32
U32 = mybir.dt.uint32
U8 = mybir.dt.uint8
FP8 = mybir.dt.float8_e4m3fn
FP8X4 = mybir.dt.float8_e4m3fn_x4
FP4X4 = mybir.dt.float4_e2m1fn_x4
ALU = mybir.AluOpType
ACT = mybir.ActivationFunctionType

P = 128
PACK = 4
KP = P * PACK
N_PASSES = N // KP
TILES = F // P


def tile_columnnormbackwardtwoproducts_kernel(
    tc, x_bytes, x_scale, g, v, m, p, a_words, a_scales, b_words, b_scales, out_0, out_1
):
    nc = tc.nc
    with ExitStack() as ctx:
        keep = ctx.enter_context(tc.tile_pool(name="keep", bufs=1))
        ring = ctx.enter_context(tc.tile_pool(name="ring", bufs=3))
        psum = ctx.enter_context(tc.psum_pool(name="psum", bufs=1))
        ctx.enter_context(tc.manual_schedule())

        def kept(name, shape, dtype):
            return keep.tile(shape, dtype, name=name, align_bytes=64)

        xs = kept("xs", [P, N_PASSES, PACK * 8], F32)
        xb = {(0, h): kept("x_byte_half%d" % h, [P, PACK, KP], U8) for h in range(2)}
        for j in range(1, N_PASSES):
            whole = kept("x_byte_tile%d" % j, [P, PACK, D], U8)
            live_x = [whole[:, :, h * KP : (h + 1) * KP] for h in range(2)]
            xb[j, 0], xb[j, 1], xb[j] = live_x[0], live_x[1], whole
        g_raw = {(fg, j): kept("g_raw%d_%d" % (fg, j), [P, PACK, KP], BF16) for fg in range(2) for j in range(N_PASSES)}
        v_sb = [kept("v_sb%d" % fg, [P, D // P, KP], BF16) for fg in range(2)]
        m_sb = kept("m_sb", [P, 2, PACK], BF16)
        p_row = kept("p_row", [P, D], BF16)
        a_w = kept("a_w", [P, 2, 2 * R], U8)
        b_w = kept("b_w", [P, 2, 2 * R], U8)
        a_s = kept("a_s", [P, 2, R], U8)
        b_s = kept("b_s", [P, 2, R], U8)
        ident_bf = kept("ident_bf", [P, P], BF16)
        ident_f32 = kept("ident_f32", [P, P], F32)
        x_codes = {(j, h): kept("x_codes%d_%d" % (j, h), [P, KP], U32) for j in range(N_PASSES) for h in range(2)}
        x_sc = {(j, h): kept("x_sc%d_%d" % (j, h), [P, KP], U8) for j in range(N_PASSES) for h in range(2)}
        g_codes = {(fg, j): kept("g_codes%d_%d" % (fg, j), [P, KP], U32) for fg in range(2) for j in range(N_PASSES)}
        g_sc = {(fg, j): kept("g_sc%d_%d" % (fg, j), [P, KP], U8) for fg in range(2) for j in range(N_PASSES)}
        vt = [kept("vt%d" % i, [P, D], BF16) for i in range(TILES)]
        c2 = kept("c2", [P, TILES], F32)
        root = kept("root", [P, TILES], F32)
        r0 = kept("r0", [P, TILES], F32)
        nh = kept("nh", [P, TILES], F32)
        nq = kept("nq", [P, TILES], F32)
        alpha = kept("alpha", [P, TILES], F32)
        alpha_m = kept("alpha_m", [P, TILES], F32)
        inv_c2 = kept("inv_c2", [P, TILES], F32)
        dots = kept("dots", [P, 2 * TILES], F32)
        neg_proj = kept("neg_proj", [P, TILES], F32)
        diag_junk = kept("diag_junk", [P, PACK, P], F32)
        up_codes = {(fg, dg): kept("up_codes%d_%d" % (fg, dg), [P, KP], U32) for fg in range(2) for dg in range(2)}
        up_sc = {(fg, dg): kept("up_sc%d_%d" % (fg, dg), [P, KP], U8) for fg in range(2) for dg in range(2)}
        dv_planes = [kept("dv_planes%d" % fg, [P, PACK, D], BF16) for fg in range(2)]
        dv_codes = {(fg, c): kept("dv_codes%d_%d" % (fg, c), [P, 256], U32) for fg in range(2) for c in range(4)}
        dv_sc = {(fg, c): kept("dv_sc%d_%d" % (fg, c), [P, 256], U8) for fg in range(2) for c in range(4)}
        n_rows = kept("n_rows", [P, 1], F32)
        root_n = kept("root_n", [P, 1], F32)
        root_nc = kept("root_nc", [P, TILES], F32)
        live = {}

        def bank_tile(b, shape, dtype):
            return psum.tile(shape, dtype, name="bank%d" % b)

        def load_x(j, h=None):
            rows = x_bytes[j * KP : (j + 1) * KP, :].rearrange("(p t) d -> p t d", t=PACK)
            if h is None:
                nc.sync.dma_start(out=xb[j][:], in_=rows)
            else:
                nc.sync.dma_start(out=xb[j, h][:], in_=rows[:, :, h * KP : (h + 1) * KP])

        def load_g(fg, j):
            rows = g[j * KP : (j + 1) * KP, fg * KP : (fg + 1) * KP]
            nc.sync.dma_start(out=g_raw[fg, j][:], in_=rows.rearrange("(p t) f -> p t f", t=PACK))

        def load_v(fg):
            cols = v[:, fg * KP : (fg + 1) * KP]
            nc.sync.dma_start(out=v_sb[fg][:], in_=cols.rearrange("(c p) f -> p c f", p=P))

        def load_weight(words, scales, w_sb, s_sb):
            nc.sync.dma_start(out=w_sb[:].bitcast(I32), in_=words.rearrange("g p n -> p g n").bitcast(I32))
            for q in range(4):
                nc.sync.dma_start(
                    out=s_sb[32 * q : 32 * q + 4, :, :].bitcast(I32),
                    in_=scales[:, 4 * q : 4 * q + 4, :].rearrange("g q n -> q g n").bitcast(I32),
                )

        def copy_on(engine, out, in_):
            if engine == "vector":
                nc.vector.tensor_copy(out=out, in_=in_)
            else:
                nc.scalar.copy(out=out, in_=in_)

        def widen(j, h, first, last, engine):
            if ("x_wide", j, h) not in live:
                live["x_wide", j, h] = ring.tile([P, PACK, KP], BF16, name="x_wide", tag="stage", bufs=6, align_bytes=64)
            for n in range(first, last):
                t, b = divmod(n, 4)
                blk = 4 * h + b
                out = live["x_wide", j, h][:, t, b * P : (b + 1) * P]
                in_ = xb[j, h][:, t, b * P : (b + 1) * P].bitcast(FP8)
                scale = xs[:, j, 8 * t + blk : 8 * t + blk + 1]
                if engine == "vector":
                    nc.vector.tensor_scalar(out=out, in0=in_, scalar1=scale, scalar2=None, op0=ALU.mult)
                else:
                    nc.scalar.activation(out=out, in_=in_, func=ACT.Copy, scale=scale)

        def weave(engine, woven, planes):
            copy_on(
                engine,
                woven.rearrange("p (c i) t -> p c t i", i=4),
                planes.rearrange("p t (c i) -> p c t i", i=4),
            )

        def weave_x(j, h, engine):
            woven = ring.tile([P, KP, PACK], BF16, name="x_woven", tag="stage", bufs=6, align_bytes=64)
            weave(engine, woven[:], live["x_wide", j, h][:])
            live["x_woven", j, h] = woven

        def quant_x(j, h):
            nc.vector.quantize_mx(
                out=x_codes[j, h][:].bitcast(FP8X4),
                scales=x_sc[j, h][:],
                in_=live["x_woven", j, h][:].rearrange("p c t -> p (c t)"),
            )

        def weave_g(fg, j, engine, s0=0, ns=PACK):
            woven = ring.tile([P, ns * P, PACK], BF16, name="g_woven", bufs=6, align_bytes=64)
            copy_on(
                engine,
                woven[:].rearrange("p (s m) t -> p m t s", s=ns),
                g_raw[fg, j][:].rearrange("p t (m s) -> p m t s", s=PACK)[:, :, :, s0 : s0 + ns],
            )
            live["g_woven", fg, j, s0] = woven

        def quant_g(fg, j, s0=0, ns=PACK):
            cols = slice(s0 * P, (s0 + ns) * P)
            nc.vector.quantize_mx(
                out=g_codes[fg, j][:, cols].bitcast(FP8X4),
                scales=g_sc[fg, j][:, cols],
                in_=live["g_woven", fg, j, s0][:].rearrange("p c t -> p (c t)"),
            )

        def turn_v(i, b):
            fg, s = divmod(i, PACK)
            bank = bank_tile(b, [P, D], BF16)
            for c in range(D // P):
                nc.tensor.transpose(bank[:, c * P : (c + 1) * P], v_sb[fg][:, c, s:KP:PACK], ident_bf[:])
            live["vt_bank", i] = bank

        def fetch_vt(i):
            nc.scalar.copy(out=vt[i][:], in_=live["vt_bank", i][:])

        def gram(fg, b):
            bank = bank_tile(b, [P, PACK, P], F32)
            for s in range(PACK):
                for c in range(D // P):
                    cols = v_sb[fg][:, c, s:KP:PACK]
                    nc.tensor.matmul(bank[:, s, :], lhsT=cols, rhs=cols, start=(c == 0), stop=(c == D // P - 1))
            live["gram", fg] = bank

        def gram_diagonal(fg):
            for s in range(PACK):
                i = PACK * fg + s
                nc.vector.scalar_tensor_tensor(
                    out=diag_junk[:, s, :], in0=live["gram", fg][:, s, :], scalar=1.0, in1=ident_bf[:],
                    op0=ALU.mult, op1=ALU.mult, accum_out=c2[:, i : i + 1],
                )

        def grad_pass(i, j):
            fg, s = divmod(i, PACK)
            for h in range(2):
                if j == 0:
                    live["grad", i, h] = bank_tile(2 * (i % 3) + h, [P, KP], F32)
                nc.tensor.matmul_mx(
                    out=live["grad", i, h][:],
                    lhsT=g_codes[fg, j][:, s * P : (s + 1) * P].bitcast(FP8X4),
                    lhsT_scale=g_sc[fg, j][:, s * P : (s + 1) * P],
                    rhs=x_codes[j, h][:].bitcast(FP8X4),
                    rhs_scale=x_sc[j, h][:],
                    start=(j == 0),
                    stop=(j == N_PASSES - 1),
                )

        def dot(i):
            resid = ring.tile([P, D], F32, name="resid", align_bytes=64)
            live["resid", i] = resid
            for h in range(2):
                cols = slice(h * KP, (h + 1) * KP)
                nc.vector.scalar_tensor_tensor(
                    out=resid[:, cols], in0=live["grad", i, h][:], scalar=-1.0, in1=vt[i][:, cols],
                    op0=ALU.mult, op1=ALU.mult, accum_out=dots[:, 2 * i + h : 2 * i + h + 1],
                )

        def projection(i):
            nc.vector.tensor_scalar(
                out=neg_proj[:, i : i + 1], in0=dots[:, 2 * i : 2 * i + 1], scalar1=dots[:, 2 * i + 1 : 2 * i + 2],
                scalar2=inv_c2[:, i : i + 1], op0=ALU.add, op1=ALU.mult,
            )

        def residual(i, h):
            cols = slice(h * KP, (h + 1) * KP)
            nc.vector.scalar_tensor_tensor(
                out=live["resid", i][:, cols], in0=vt[i][:, cols], scalar=neg_proj[:, i : i + 1],
                in1=live["grad", i, h][:], op0=ALU.mult, op1=ALU.add,
            )

        def make_up(i):
            up_t = ring.tile([P, D], BF16, name="up_t", align_bytes=64)
            for h in range(2):
                cols = slice(h * KP, (h + 1) * KP)
                nc.vector.scalar_tensor_tensor(
                    out=up_t[:, cols], in0=live["resid", i][:, cols], scalar=alpha[:, i : i + 1], in1=p_row[:, cols],
                    op0=ALU.mult, op1=ALU.mult,
                )
            live["up_t", i] = up_t

        def turn_up(i):
            words = live["up_t", i][:].bitcast(F32)
            bank = bank_tile(6, [P, PACK, P], F32)
            for dg in range(2):
                for u in range(2):
                    nc.tensor.transpose(bank[:, 2 * dg + u, :], words[:, 256 * dg + u : 256 * (dg + 1) : 2], ident_f32[:])
            live["up_bank", i] = bank

        def fetch_up(i):
            woven = ring.tile([P, 2, KP], BF16, name="up_woven", align_bytes=64)
            nc.scalar.copy(
                out=woven[:].bitcast(F32).rearrange("p g (f u) -> p g f u", u=2),
                in_=live["up_bank", i][:].rearrange("p (g u) f -> p g f u", u=2),
            )
            live["up_woven", i] = woven

        def quant_up(i):
            fg, s = divmod(i, PACK)
            for dg in range(2):
                nc.vector.quantize_mx(
                    out=up_codes[fg, dg][:, s * P : (s + 1) * P].bitcast(FP8X4),
                    scales=up_sc[fg, dg][:, s * P : (s + 1) * P],
                    in_=live["up_woven", i][:, dg, :],
                )

        def make_dv(i, first, last):
            fg, s = divmod(i, PACK)
            cols = slice(first, last)
            nc.scalar.activation(
                out=dv_planes[fg][:, s, cols], in_=live["resid", i][:, cols], func=ACT.Copy, scale=alpha_m[:, i : i + 1]
            )

        def weave_dv(fg, c, engine):
            woven = ring.tile([P, 256, PACK], BF16, name="dv_woven", bufs=4, align_bytes=64)
            weave(engine, woven[:], dv_planes[fg][:, :, 256 * c : 256 * (c + 1)])
            live["dv_woven", fg, c] = woven

        def turn_dv(fg, c, b):
            bank = bank_tile(b, [P, 256 * PACK], BF16)
            for e in range(2):
                cols = slice(256 * c + P * e, 256 * c + P * (e + 1))
                nc.tensor.matmul(
                    bank[:, e * KP : (e + 1) * KP], lhsT=ident_bf[:],
                    rhs=dv_planes[fg][:, :, cols].rearrange("p t c -> p c t"), start=True, stop=True,
                )
            live["dv_bank", fg, c] = bank

        def fetch_dv(fg, c):
            woven = ring.tile([P, 256, PACK], BF16, name="dv_woven", bufs=4, align_bytes=64)
            nc.scalar.copy(out=woven[:].rearrange("p c t -> p (c t)"), in_=live["dv_bank", fg, c][:])
            live["dv_woven", fg, c] = woven

        def quant_dv(fg, c):
            nc.vector.quantize_mx(
                out=dv_codes[fg, c][:].bitcast(FP8X4),
                scales=dv_sc[fg, c][:],
                in_=live["dv_woven", fg, c][:].rearrange("p c t -> p (c t)"),
            )

        def db_product(fg, b):
            for rh in range(2):
                bank = bank_tile(b + rh, [P, KP], F32)
                for dg in range(2):
                    nc.tensor.matmul_mx(
                        out=bank[:],
                        lhsT=a_w[:, dg, 2 * P * rh : 2 * P * (rh + 1)].bitcast(FP4X4),
                        lhsT_scale=a_s[:, dg, P * rh : P * (rh + 1)],
                        rhs=up_codes[fg, dg][:].bitcast(FP8X4),
                        rhs_scale=up_sc[fg, dg][:],
                        start=(dg == 0),
                        stop=(dg == 1),
                    )
                live["db", fg, rh] = bank

        def scale_out(engine, out, in_):
            if engine == "vector":
                nc.vector.tensor_scalar(out=out, in0=in_, scalar1=SCALE, scalar2=None, op0=ALU.mult)
            else:
                nc.scalar.activation(out=out, in_=in_, func=ACT.Copy, scale=SCALE)

        def db_store(fg, rh, engine):
            res = ring.tile([P, P, PACK], F32, name="result", tag="stage", bufs=6, align_bytes=64)
            scale_out(engine, res[:], live["db", fg, rh][:].rearrange("p (s m) -> p m s", s=PACK))
            nc.sync.dma_start(
                out=out_1[rh * P : (rh + 1) * P, fg * KP : (fg + 1) * KP], in_=res[:].rearrange("p m s -> p (m s)")
            )

        def da_product(c):
            bank = bank_tile(c, [P, 2, R], F32)
            for e in range(2):
                for rh in range(2):
                    for fg in range(2):
                        nc.tensor.matmul_mx(
                            out=bank[:, e, P * rh : P * (rh + 1)],
                            lhsT=dv_codes[fg, c][:, e * P : (e + 1) * P].bitcast(FP8X4),
                            lhsT_scale=dv_sc[fg, c][:, e * P : (e + 1) * P],
                            rhs=b_w[:, fg, 2 * P * rh : 2 * P * (rh + 1)].bitcast(FP4X4),
                            rhs_scale=b_s[:, fg, P * rh : P * (rh + 1)],
                            start=(fg == 0),
                            stop=(fg == 1),
                        )
            live["da", c] = bank

        def da_store(c, engine):
            res = ring.tile([P, 2, R], F32, name="result", tag="stage", bufs=6, align_bytes=64)
            scale_out(engine, res[:], live["da", c][:])
            nc.sync.dma_start(out=out_0[256 * c : 256 * (c + 1), :].rearrange("(e p) r -> p e r", p=P), in_=res[:])

        def load_small(k):
            if k == 0:
                nc.sync.dma_start(out=xs[:], in_=x_scale.rearrange("(j p t) b -> p j (t b)", p=P, t=PACK))
            if k == 1:
                nc.sync.dma_start(out=m_sb[:], in_=m.rearrange("(g p s) -> p g s", p=P, s=PACK))
            if k == 2:
                nc.sync.dma_start(out=p_row[:], in_=p.partition_broadcast(P))
            if k == 3:
                load_weight(a_words, a_scales, a_w, a_s)
                load_weight(b_words, b_scales, b_w, b_s)

        def norm(k):
            if k == 0:
                nc.scalar.activation(out=root[:], in_=c2[:], func=ACT.Sqrt)
            if k == 1:
                nc.scalar.activation(out=root_nc[:], in_=root[:], func=ACT.Copy, scale=root_n[:])
            if k == 2:
                nc.vector.reciprocal(out=inv_c2[:], in_=c2[:])
            if k == 3:
                nc.vector.reciprocal(out=r0[:], in_=root_nc[:])
            if k == 4:
                nc.vector.scalar_tensor_tensor(out=nh[:], in0=c2[:], scalar=-0.5 * N, in1=r0[:], op0=ALU.mult, op1=ALU.mult)
            if k == 5:
                nc.vector.tensor_tensor(out=nq[:], in0=nh[:], in1=r0[:], op=ALU.mult)
            if k == 6:
                nc.vector.scalar_tensor_tensor(out=alpha[:], in0=nq[:], scalar=1.5, in1=r0[:], op0=ALU.add, op1=ALU.mult)
            if k == 7:
                nc.vector.tensor_tensor(out=alpha_m[:], in0=alpha[:], in1=m_sb[:].rearrange("p g s -> p (g s)"), op=ALU.mult)

        nc.vector.memset(n_rows[:], float(N))
        nc.scalar.activation(out=root_n[:], in_=n_rows[:], func=ACT.Sqrt)
        make_identity(nc, ident_bf[:])
        make_identity(nc, ident_f32[:])
        nc.gpsimd.memset(a_s[:].bitcast(I32), 0)
        nc.gpsimd.memset(b_s[:].bitcast(I32), 0)
        load_small(0)
        load_x(0, 0)
        load_g(0, 0)
        load_x(0, 1)
        load_x(1)
        load_v(0)
        load_g(0, 1)
        load_x(2)
        load_g(0, 2)
        load_v(1)
        load_x(3)
        load_g(0, 3)
        load_small(1)
        for j in range(N_PASSES):
            load_g(1, j)
        load_small(2)
        load_small(3)
        widen(0, 0, 8, 16, "vector")
        turn_v(1, 7)
        weave_g(0, 0, "vector", 0, 2)
        widen(0, 0, 0, 8, "scalar")
        weave_x(0, 0, "vector")
        widen(0, 1, 0, 16, "scalar")
        quant_x(0, 0)
        quant_g(0, 0, 0, 2)
        weave_x(0, 1, "vector")
        widen(1, 0, 0, 16, "scalar")
        weave_g(0, 1, "vector", 0, 2)
        quant_x(0, 1)
        weave_x(1, 0, "vector")
        quant_g(0, 1, 0, 2)
        widen(1, 1, 0, 16, "scalar")
        quant_x(1, 0)
        weave_x(1, 1, "vector")
        weave_g(0, 2, "vector", 0, 2)
        widen(2, 0, 0, 16, "scalar")
        grad_pass(1, 0)
        quant_x(1, 1)
        weave_x(2, 0, "vector")
        widen(2, 1, 0, 16, "scalar")
        weave_g(0, 3, "vector", 0, 2)
        gram(0, 4)
        gram_diagonal(0)
        weave_x(2, 1, "vector")
        quant_x(2, 0)
        gram(1, 5)
        turn_v(0, 6)
        quant_x(2, 1)
        grad_pass(0, 0)
        quant_g(0, 3, 0, 2)
        widen(3, 0, 0, 16, "scalar")
        quant_g(0, 2, 0, 2)
        gram_diagonal(1)
        weave_x(3, 0, "vector")
        widen(3, 1, 0, 16, "scalar")
        weave_x(3, 1, "vector")
        fetch_vt(1)
        grad_pass(0, 1)
        turn_v(3, 7)
        weave_g(0, 0, "scalar", 2, 2)
        quant_x(3, 0)
        norm(0)
        grad_pass(0, 2)
        quant_x(3, 1)
        weave_g(0, 1, "scalar", 2, 2)
        grad_pass(0, 3)
        norm(1)
        grad_pass(1, 1)
        quant_g(0, 0, 2, 2)
        grad_pass(1, 2)
        norm(3)
        norm(2)
        fetch_vt(0)
        quant_g(0, 1, 2, 2)
        weave_g(0, 2, "scalar", 2, 2)
        grad_pass(1, 3)
        norm(4)
        dot(0)
        weave_g(0, 3, "scalar", 2, 2)
        weave_g(1, 0, "scalar", 0, 2)
        weave_g(1, 1, "scalar", 0, 2)
        turn_v(2, 6)
        norm(5)
        weave_g(1, 2, "scalar", 0, 2)
        grad_pass(2, 0)
        quant_g(0, 2, 2, 2)
        projection(0)
        dot(1)
        fetch_vt(3)
        fetch_vt(2)
        residual(0, 0)
        projection(1)
        residual(0, 1)
        grad_pass(2, 1)
        quant_g(0, 3, 2, 2)
        residual(1, 0)
        grad_pass(2, 2)
        norm(6)
        grad_pass(2, 3)
        grad_pass(3, 0)
        weave_g(1, 3, "scalar", 0, 2)
        quant_g(1, 0, 0, 2)
        quant_g(1, 1, 0, 2)
        norm(7)
        turn_v(4, 7)
        make_up(0)
        residual(1, 1)
        dot(2)
        fetch_vt(4)
        make_up(1)
        grad_pass(3, 1)
        grad_pass(3, 2)
        projection(2)
        make_dv(0, 0, 1024)
        weave_g(1, 0, "scalar", 2, 2)
        make_dv(1, 0, 1024)
        grad_pass(3, 3)
        weave_g(1, 1, "scalar", 2, 2)
        dot(3)
        grad_pass(4, 0)
        turn_up(0)
        grad_pass(4, 1)
        turn_v(5, 7)
        residual(2, 0)
        projection(3)
        quant_g(1, 2, 0, 2)
        residual(2, 1)
        grad_pass(5, 0)
        grad_pass(5, 1)
        make_up(2)
        fetch_up(0)
        residual(3, 0)
        quant_g(1, 3, 0, 2)
        residual(3, 1)
        fetch_vt(5)
        weave_g(1, 2, "scalar", 2, 2)
        weave_g(1, 3, "scalar", 2, 2)
        grad_pass(4, 2)
        grad_pass(5, 2)
        grad_pass(4, 3)
        grad_pass(5, 3)
        make_dv(2, 0, 1024)
        make_up(3)
        quant_g(1, 2, 2, 2)
        make_dv(3, 0, 1024)
        turn_v(6, 7)
        quant_g(1, 0, 2, 2)
        turn_up(1)
        grad_pass(6, 0)
        fetch_up(1)
        quant_g(1, 1, 2, 2)
        dot(4)
        dot(5)
        quant_g(1, 3, 2, 2)
        fetch_vt(6)
        weave_dv(0, 0, "scalar")
        grad_pass(6, 1)
        grad_pass(6, 2)
        projection(4)
        turn_up(2)
        weave_dv(0, 1, "scalar")
        quant_up(1)
        quant_up(0)
        projection(5)
        residual(4, 1)
        residual(4, 0)
        make_dv(4, 0, 1024)
        fetch_up(2)
        turn_v(7, 7)
        grad_pass(6, 3)
        fetch_vt(7)
        grad_pass(7, 0)
        grad_pass(7, 1)
        residual(5, 1)
        turn_up(3)
        make_up(4)
        grad_pass(7, 2)
        grad_pass(7, 3)
        residual(5, 0)
        make_dv(5, 0, 1024)
        quant_dv(0, 1)
        fetch_up(3)
        dot(6)
        make_up(5)
        quant_dv(0, 0)
        dot(7)
        weave_dv(0, 2, "scalar")
        projection(6)
        quant_up(2)
        turn_up(4)
        fetch_up(4)
        quant_up(3)
        residual(6, 0)
        residual(6, 1)
        weave_dv(0, 3, "scalar")
        turn_up(5)
        projection(7)
        quant_dv(0, 3)
        make_up(6)
        fetch_up(5)
        residual(7, 0)
        make_dv(6, 0, 1024)
        turn_up(6)
        make_dv(7, 0, 512)
        fetch_up(6)
        db_product(0, 4)
        residual(7, 1)
        make_up(7)
        weave_dv(1, 0, "vector")
        turn_up(7)
        weave_dv(1, 1, "vector")
        quant_dv(1, 0)
        da_product(0)
        make_dv(7, 512, 1024)
        db_store(0, 0, "scalar")
        quant_dv(0, 2)
        quant_dv(1, 1)
        da_product(1)
        weave_dv(1, 2, "vector")
        quant_up(4)
        db_store(0, 1, "scalar")
        quant_up(6)
        quant_dv(1, 2)
        quant_up(5)
        weave_dv(1, 3, "scalar")
        fetch_up(7)
        quant_dv(1, 3)
        da_product(2)
        da_product(3)
        quant_up(7)
        da_store(0, "scalar")
        da_store(1, "vector")
        da_store(2, "scalar")
        da_store(3, "vector")
        db_product(1, 6)
        db_store(1, 0, "scalar")
        db_store(1, 1, "vector")
